import numpy as np
import ml_dtypes


def mxq(x, axis, fmt="e4m3"):
    dtype, down = {"e4m3": (ml_dtypes.float8_e4m3fn, 7), "e5m2": (ml_dtypes.float8_e5m2, 14)}[fmt]
    v = np.moveaxis(np.asarray(x, np.float32).astype(ml_dtypes.bfloat16).astype(np.float64), axis, -1)
    blocks = v.reshape(v.shape[:-1] + (-1, 32))
    amax = np.abs(blocks).max(-1, keepdims=True)
    byte = np.maximum(np.where(amax > 0, np.frexp(amax)[1] - 1 + 127, 0) - down, 1)
    scale = np.exp2(byte - 127.0)
    codes = (blocks / scale).astype(np.float32).astype(dtype).astype(np.float64)
    return np.moveaxis((codes * scale).reshape(v.shape), -1, axis)


WIDE = False


def mx_kscale(k):
    if not WIDE:
        return np.ones(k)
    levels = np.array([30, -30])
    if k % 512:
        return np.exp2(np.random.permutation(np.resize(levels, k // 32))).repeat(32)
    a = np.empty((k // 512, 16))
    for p in range(k // 512):
        a[p, :8] = np.random.permutation(np.resize(levels, 8))
        for g in range(8):
            far = levels[np.abs(levels - a[p, g]) >= 10]
            a[p, g + 8] = far[np.random.randint(len(far))]
    return np.exp2(a.ravel()).repeat(32)


def f64(x):
    return np.asarray(x).astype(np.float64)


def striped(idx):
    return np.tile(np.asarray(idx).reshape(-1, 16).T, (8, 1)).astype(np.uint16)


def unstriped(offs):
    return offs[:16].T.reshape(-1).astype(np.int64)


E2M1 = np.array([0.0, 0.5, 1.0, 1.5, 2.0, 3.0, 4.0, 6.0, -0.0, -0.5, -1.0, -1.5, -2.0, -3.0, -4.0, -6.0])


def pack_weight(w, fmt):
    k, n = w.shape
    w = f64(np.asarray(w, np.float32).astype(ml_dtypes.bfloat16)).reshape(k // 32, 32, n)
    amax = np.abs(w).max(1)
    if fmt in ("e4m3", "e5m2"):
        byte = np.frexp(amax)[1] - 1 + 127 - (7 if fmt == "e4m3" else 14)
    else:
        mant, ex = np.frexp(amax / 6.0)
        byte = np.where(mant > 0.5, ex, ex - 1) + 127
    byte = np.clip(np.where(amax > 0, byte, 1), 1, 254)
    scaled = (w * np.exp2(127.0 - byte)[:, None, :]).reshape(k, n).astype(np.float32)
    by_word = np.ascontiguousarray(scaled.reshape(k // 512, 128, 4, n).transpose(0, 1, 3, 2))
    if fmt in ("e4m3", "e5m2"):
        words = by_word.astype(ml_dtypes.float8_e4m3fn if fmt == "e4m3" else ml_dtypes.float8_e5m2).view(np.uint8)
    else:
        c = by_word.astype(ml_dtypes.float4_e2m1fn).view(np.uint8) & 0xF
        words = (c[..., 0::2] | (c[..., 1::2] << 4)).reshape(k // 512, 128, 2 * n)
    return np.ascontiguousarray(words), np.ascontiguousarray(byte.astype(np.uint8).reshape(k // 512, 16, n))


def unpack_weight(words, scales, fmt):
    g, _, n = scales.shape
    words = np.ascontiguousarray(words).reshape(g, 128, n, -1)
    if fmt in ("e4m3", "e5m2"):
        vals = words.view(ml_dtypes.float8_e4m3fn if fmt == "e4m3" else ml_dtypes.float8_e5m2).astype(np.float64)
    else:
        nib = np.empty((g, 128, n, 4), np.uint8)
        nib[..., 0::2] = words & 0xF
        nib[..., 1::2] = words >> 4
        vals = E2M1[nib]
    vals = vals * np.repeat(np.exp2(scales.astype(np.float64) - 127.0), 8, axis=1)[..., None]
    return vals.transpose(0, 1, 3, 2).reshape(g * 512, n)


def sigmoid(v):
    return 1.0 / (1.0 + np.exp(-v))


K, T, Z, J, R, C, O, N, E = 512, 1024, 1024, 256, 512, 512, 256, 256, 1024


def setup_inputs():
    n = np.random.standard_normal
    idx = np.random.permutation(T)[:J]
    idx2 = np.random.permutation(Z)[:J]
    idx3 = np.random.permutation(C)[:J]
    idx4 = np.random.permutation(C)[:J]
    idx5 = np.random.permutation(C)[:O]
    idx6 = np.random.permutation(E)[:O]
    fk = mx_kscale(K)
    fr = mx_kscale(R)
    xtp = pack_weight(n((K, T)) / fk[:, None], "e4m3")
    xop = pack_weight(n((K, Z)) / fk[:, None], "e2m1")
    wp = pack_weight(n((K, R)) * 1 / np.sqrt(K) * fk[:, None] * fr, "e5m2")
    w2p = pack_weight(n((K, R)) * 1 / np.sqrt(K) * fk[:, None] * fr, "e5m2")
    wbp = pack_weight(n((R, N)) * 1 / np.sqrt(R) / fr[:, None], "e5m2")
    return {
        "xt_words": xtp[0],
        "xt_scales": xtp[1],
        "xo_words": xop[0],
        "xo_scales": xop[1],
        "w_words": wp[0],
        "w_scales": wp[1],
        "w2_words": w2p[0],
        "w2_scales": w2p[1],
        "wb_words": wbp[0],
        "wb_scales": wbp[1],
        "tz": (n((N, E))).astype(np.float32),
        "so": (np.random.uniform(0.6, 1.6, (N, 1))).astype(np.float32),
        "bo": (np.random.uniform(-1.0, 1.0, (N, 1))).astype(np.float32),
        "offs": striped(idx),
        "offs2": striped(idx2),
        "offs3": striped(idx3),
        "offs4": striped(idx4),
        "offs5": striped(idx5),
        "offs6": striped(idx6),
    }


def reference(xt_words, xt_scales, xo_words, xo_scales, w_words, w_scales, w2_words, w2_scales, wb_words, wb_scales, tz, so, bo, offs, offs2, offs3, offs4, offs5, offs6):
    idx = unstriped(offs)
    idx2 = unstriped(offs2)
    idx3 = unstriped(offs3)
    idx4 = unstriped(offs4)
    idx5 = unstriped(offs5)
    idx6 = unstriped(offs6)
    xtu = unpack_weight(xt_words, xt_scales, "e4m3")
    xou = unpack_weight(xo_words, xo_scales, "e2m1")
    wu = unpack_weight(w_words, w_scales, "e5m2")
    w2u = unpack_weight(w2_words, w2_scales, "e5m2")
    wbu = unpack_weight(wb_words, wb_scales, "e5m2")
    xtidxg = xtu[:, idx]
    xoidx2g = xou[:, idx2]
    a = wu.T @ xtidxg + w2u.T @ xoidx2g
    b = w2u.T @ xtidxg + wu.T @ xoidx2g
    pw = np.zeros((R, C))
    pw[:, idx3] = a
    pv = np.zeros((R, C))
    pv[:, idx4] = b
    pg = pw + pv
    hid = pg[:, idx5]
    hidq = mxq(hid, 0, "e4m3")
    p = wbu.T @ hidq
    y = p * sigmoid(f64(tz)[:, idx6] * f64(so) + f64(bo))
    return y

@@ -1,0 +1,206 @@
+from contextlib import ExitStack
+
+import concourse.mybir as mybir
+
+K, T, Z, J, R, C, O, N, E = 512, 1024, 1024, 256, 512, 512, 256, 256, 1024
+FLOPS = 2 * (4 * K * R * J + R * N * O)
+
+F32 = mybir.dt.float32
+BF16 = mybir.dt.bfloat16
+I32 = mybir.dt.int32
+U32 = mybir.dt.uint32
+U16 = mybir.dt.uint16
+U8 = mybir.dt.uint8
+E4M3 = mybir.dt.float8_e4m3fn_x4
+E5M2 = mybir.dt.float8_e5m2_x4
+E2M1 = mybir.dt.float4_e2m1fn_x4
+ACT = mybir.ActivationFunctionType
+ALU = mybir.AluOpType
+
+P = 128
+PACK = 4
+QUADS = 4
+
+
+def tile_list_crossed_shared_one_finalgate_kernel(
+    tc, xt_words, xt_scales, xo_words, xo_scales, w_words, w_scales, w2_words, w2_scales,
+    wb_words, wb_scales, tz, so, bo, offs, offs2, offs3, offs4, offs5, offs6, out,
+):
+    nc = tc.nc
+    with ExitStack() as ctx:
+        keep = ctx.enter_context(tc.tile_pool(name="keep", bufs=1))
+        ring = ctx.enter_context(tc.tile_pool(name="ring", bufs=2))
+        psum = ctx.enter_context(tc.psum_pool(name="psum", bufs=1))
+
+        def load_list(src, name):
+            tile = keep.tile([P, J // 16], U16, name=name)
+            nc.sync.dma_start(tile[:], src)
+            return tile
+
+        def zeroed_scales(width, name):
+            tile = keep.tile([P, width], U8, name=name, align_bytes=64)
+            nc.vector.memset(tile[:].bitcast(I32), 0)
+            return tile
+
+        def load_scales(queue, tile, src):
+            for q in range(QUADS):
+                queue.dma_start(tile[32 * q : 32 * q + 4, :].bitcast(I32), src[0, 4 * q : 4 * q + 4, :].bitcast(I32))
+
+        def load_words(src, width, name, tag):
+            tile = keep.tile([P, width], U32, name=name, tag=tag, align_bytes=64)
+            nc.sync.dma_start(tile[:].bitcast(I32), src[0].rearrange("p n t -> p (n t)").bitcast(I32))
+            return tile
+
+        xo_s = zeroed_scales(Z, "xo_s")
+        xt_s = zeroed_scales(T, "xt_s")
+        w_s = zeroed_scales(R, "w_s")
+        w2_s = zeroed_scales(R, "w2_s")
+        wb_s = zeroed_scales(N, "wb_s")
+
+        note_list = load_list(offs2, "note_list")
+        load_scales(nc.sync, xo_s, xo_scales)
+        token_list = load_list(offs, "token_list")
+        xo_w = keep.tile([P, Z], U16, name="xo_w", tag="table1", align_bytes=64)
+        nc.sync.dma_start(xo_w[:].bitcast(I32), xo_words[0].bitcast(I32))
+        xt_w = load_words(xt_words, T, "xt_w", "table0")
+        load_scales(nc.sync, xt_s, xt_scales)
+        w_w = load_words(w_words, R, "w_w", "w_w")
+        w2_w = load_words(w2_words, R, "w2_w", "w2_w")
+        load_scales(nc.sync, w_s, w_scales)
+        load_scales(nc.sync, w2_s, w2_scales)
+        a_list = load_list(offs3, "a_list")
+        b_list = load_list(offs4, "b_list")
+        read_list = load_list(offs5, "read_list")
+        wb_w = load_words(wb_words, N, "wb_w", "wb_w")
+        load_scales(nc.sync, wb_s, wb_scales)
+        gate_list = load_list(offs6, "gate_list")
+        slope = keep.tile([P, 2], F32, name="slope")
+        offset = keep.tile([P, 2], F32, name="offset")
+        with nc.allow_non_contiguous_dma(reason="one value a partition and half"):
+            nc.sync.dma_start(slope[:], so.rearrange("(h p) o -> p (h o)", p=P))
+            nc.sync.dma_start(offset[:], bo.rearrange("(h p) o -> p (h o)", p=P))
+
+        a_boards = [keep.tile([P, C], F32, name=f"a_board{i}") for i in range(3)]
+        b_boards = [keep.tile([P, C], F32, name=f"b_board{i}") for i in range(3)]
+        for pair in zip(a_boards, b_boards):
+            for board in pair:
+                nc.vector.memset(board[:], 0.0)
+
+        xo_gw = keep.tile([P, J], U16, name="xo_gw", align_bytes=64)
+        xo_gs = keep.tile([P, J], U8, name="xo_gs", align_bytes=64)
+        xt_gw = keep.tile([P, J], U32, name="xt_gw", align_bytes=64)
+        xt_gs = keep.tile([P, J], U8, name="xt_gs", align_bytes=64)
+        nc.vector.tensor_copy(xo_gs[:], xo_s[:].indirect(note_list[:]))
+        nc.vector.tensor_copy(xo_gw[:], xo_w[:].indirect(note_list[:]))
+        nc.vector.tensor_copy(xt_gw[:], xt_w[:].indirect(token_list[:]))
+        nc.vector.tensor_copy(xt_gs[:], xt_s[:].indirect(token_list[:]))
+
+        def dealt(copy, src, dtype, run, name):
+            tile = keep.tile([P, PACK, P], dtype, name=name, align_bytes=64)
+            copy(
+                tile[:].rearrange("p t (b i) -> p b t i", i=run),
+                src[:].rearrange("p (b i t) -> p b t i", i=run, t=PACK),
+            )
+            return tile
+
+        w_dw = dealt(nc.scalar.copy, w_w, U32, 4, "w_dw")
+        w2_dw = dealt(nc.scalar.copy, w2_w, U32, 4, "w2_dw")
+        w_ds = dealt(nc.vector.tensor_copy, w_s, U8, 16, "w_ds")
+        w2_ds = dealt(nc.vector.tensor_copy, w2_s, U8, 16, "w2_ds")
+
+        tz_rows = []
+        for h in range(2):
+            rows = keep.tile([P, E], F32, name=f"tz{h}", tag=f"table{h}", align_bytes=64)
+            nc.sync.dma_start(rows[:], tz[P * h : P * (h + 1), :])
+            tz_rows.append(rows)
+
+        def crossed(t, token_w, token_s, note_w, note_s, name):
+            acc = psum.tile([P, J], F32, name=name, tag="first", bufs=6)
+            passes = [(token_w, token_s, xt_gw[:].bitcast(E4M3), xt_gs), (note_w, note_s, xo_gw[:].bitcast(E2M1), xo_gs)]
+            if token_w is w2_dw:
+                passes = passes[::-1]
+            for n, (lw, ls, rw, rs) in enumerate(passes):
+                nc.tensor.matmul_mx(
+                    acc[:], lhsT=lw[:, t, :].bitcast(E5M2), lhsT_scale=ls[:, t, :],
+                    rhs=rw, rhs_scale=rs[:], start=(n == 0), stop=(n == 1),
+                )
+            sb = keep.tile([P, J], F32, name=name + "_sb")
+            nc.scalar.copy(sb[:], acc[:])
+            return sb
+
+        def first_a(t):
+            return crossed(t, w_dw, w_ds, w2_dw, w2_ds, f"a{t}")
+
+        def first_b(t):
+            return crossed(t, w2_dw, w2_ds, w_dw, w_ds, f"b{t}")
+
+        def put_scalar(board, lst, src, lo, hi):
+            nc.scalar.activation(board[:].indirect(lst[:, lo // 16 : hi // 16]), src[:, lo:hi], ACT.Copy)
+
+        def put_vector(board, lst, src, lo, hi):
+            nc.vector.tensor_copy(board[:].indirect(lst[:, lo // 16 : hi // 16]), src[:, lo:hi])
+
+        hid = keep.tile([P, O, PACK], BF16, name="hid", align_bytes=64)
+        pages = {}
+
+        def join(t, engine):
+            pages[t] = keep.tile([P, C], F32, name=f"page{t}")
+            engine.tensor_tensor(pages[t][:], a_boards[t % 3][:], b_boards[t % 3][:], ALU.add)
+
+        def read(t, lo, hi):
+            nc.vector.tensor_copy(hid[:, lo:hi, t], pages[t][:].indirect(read_list[:, lo // 16 : hi // 16]))
+
+        a0 = first_a(0)
+        b0 = first_b(0)
+        put_vector(a_boards[0], a_list, a0, 0, J)
+        a1 = first_a(1)
+        put_scalar(b_boards[0], b_list, b0, 0, J)
+        put_vector(a_boards[1], a_list, a1, 0, J)
+        b1 = first_b(1)
+        a2 = first_a(2)
+        put_scalar(b_boards[1], b_list, b1, 0, J)
+        join(0, nc.vector)
+        put_vector(a_boards[2], a_list, a2, 0, J)
+        read(0, 0, O)
+        b2 = first_b(2)
+        a3 = first_a(3)
+        put_scalar(b_boards[2], b_list, b2, 0, J)
+        join(1, nc.vector)
+        b3 = first_b(3)
+        put_scalar(a_boards[0], a_list, a3, 0, P)
+        read(1, 0, O)
+        put_scalar(b_boards[0], b_list, b3, 0, J)
+        join(2, nc.vector)
+        put_vector(a_boards[0], a_list, a3, P, J)
+        read(2, 0, O)
+        join(3, nc.vector)
+
+
+        gate = keep.tile([P, 2, O], F32, name="gate")
+        for h in range(2):
+            nc.scalar.activation(
+                gate[:, h, :], tz_rows[h][:].indirect(gate_list[:]), ACT.Sigmoid,
+                bias=offset[:, h : h + 1], scale=slope[:, h : h + 1],
+            )
+        out_rows = out.rearrange("(h p) o -> p h o", p=P)
+        read(3, 0, P)
+        read(3, P, O)
+        accs = []
+        for u in range(2):
+            cols = slice(P * u, P * (u + 1))
+            hid_w = keep.tile([P, P], U32, name=f"hid_w{u}", align_bytes=64)
+            hid_s = keep.tile([P, P], U8, name=f"hid_s{u}", align_bytes=64)
+            nc.vector.quantize_mx(hid_w[:].bitcast(E4M3), hid_s[:], hid[:, cols, :].rearrange("p o t -> p (o t)"))
+            acc = psum.tile([P, 2, P], F32, name=f"p{u}", tag="second", bufs=2)
+            for h in range(2):
+                rows = slice(P * h, P * (h + 1))
+                nc.tensor.matmul_mx(
+                    acc[:, h, :], lhsT=wb_w[:, rows].bitcast(E5M2), lhsT_scale=wb_s[:, rows],
+                    rhs=hid_w[:].bitcast(E4M3), rhs_scale=hid_s[:], start=True, stop=True,
+                )
+            accs.append(acc)
+        for u in range(2):
+            cols = slice(P * u, P * (u + 1))
+            y = keep.tile([P, 2, P], F32, name=f"y{u}")
+            nc.vector.tensor_tensor(y[:], accs[u][:], gate[:, :, cols], ALU.mult)
+            (nc.sync, nc.scalar)[u].dma_start(out_rows[:, :, cols], y[:])

@@ -51,6 +51,11 @@ def tile_list_crossed_shared_one_finalgate_kernel(
             nc.sync.dma_start(tile[:].bitcast(I32), src[0].rearrange("p n t -> p (n t)").bitcast(I32))
             return tile
 
+        warm_in = keep.tile([P, 1], F32, name="warm_in")
+        warm_out = keep.tile([P, 1], F32, name="warm_out")
+        nc.gpsimd.memset(warm_in[:], 0.0)
+        nc.scalar.activation(warm_out[:], warm_in[:], ACT.Sigmoid)
+
         xo_s = zeroed_scales(Z, "xo_s")
         xt_s = zeroed_scales(T, "xt_s")
         w_s = zeroed_scales(R, "w_s")

@@ -51,11 +51,6 @@ def tile_list_crossed_shared_one_finalgate_kernel(
             nc.sync.dma_start(tile[:].bitcast(I32), src[0].rearrange("p n t -> p (n t)").bitcast(I32))
             return tile
 
-        warm_in = keep.tile([P, 1], F32, name="warm_in")
-        warm_out = keep.tile([P, 1], F32, name="warm_out")
-        nc.gpsimd.memset(warm_in[:], 0.0)
-        nc.scalar.activation(warm_out[:], warm_in[:], ACT.Sigmoid)
-
         xo_s = zeroed_scales(Z, "xo_s")
         xt_s = zeroed_scales(T, "xt_s")
         w_s = zeroed_scales(R, "w_s")
@@ -111,7 +106,11 @@ def tile_list_crossed_shared_one_finalgate_kernel(
         w_dw = dealt(nc.scalar.copy, w_w, U32, 4, "w_dw")
         w2_dw = dealt(nc.scalar.copy, w2_w, U32, 4, "w2_dw")
         w_ds = dealt(nc.vector.tensor_copy, w_s, U8, 16, "w_ds")
-        w2_ds = dealt(nc.vector.tensor_copy, w2_s, U8, 16, "w2_ds")
+        w2_ds = keep.tile([P, PACK, P], U8, name="w2_ds", align_bytes=64)
+        w2_cols = w2_s[:].rearrange("p (b i t) -> p b t i", i=16, t=PACK)
+        w2_dealt = w2_ds[:].rearrange("p t (b i) -> p b t i", i=16)
+        nc.vector.tensor_copy(w2_dealt[:, :, 0:1, :], w2_cols[:, :, 0:1, :])
+        nc.vector.tensor_copy(w2_dealt[:, :, 1:PACK, :], w2_cols[:, :, 1:PACK, :])
 
         tz_rows = []
         for h in range(2):
@@ -119,8 +118,8 @@ def tile_list_crossed_shared_one_finalgate_kernel(
             nc.sync.dma_start(rows[:], tz[P * h : P * (h + 1), :])
             tz_rows.append(rows)
 
-        def crossed(t, token_w, token_s, note_w, note_s, name):
-            acc = psum.tile([P, J], F32, name=name, tag="first", bufs=6)
+        def crossed(t, token_w, token_s, note_w, note_s, name, copy):
+            acc = psum.tile([P, J], F32, name=name, tag="first", bufs=3)
             passes = [(token_w, token_s, xt_gw[:].bitcast(E4M3), xt_gs), (note_w, note_s, xo_gw[:].bitcast(E2M1), xo_gs)]
             if token_w is w2_dw:
                 passes = passes[::-1]
@@ -129,15 +128,15 @@ def tile_list_crossed_shared_one_finalgate_kernel(
                     acc[:], lhsT=lw[:, t, :].bitcast(E5M2), lhsT_scale=ls[:, t, :],
                     rhs=rw, rhs_scale=rs[:], start=(n == 0), stop=(n == 1),
                 )
-            sb = keep.tile([P, J], F32, name=name + "_sb")
-            nc.scalar.copy(sb[:], acc[:])
+            sb = keep.tile([P, J], F32, name=name + "_sb", tag=name + "_sb")
+            copy(sb[:], acc[:])
             return sb
 
-        def first_a(t):
-            return crossed(t, w_dw, w_ds, w2_dw, w2_ds, f"a{t}")
+        def first_a(t, copy=nc.scalar.copy):
+            return crossed(t, w_dw, w_ds, w2_dw, w2_ds, f"a{t}", copy)
 
         def first_b(t):
-            return crossed(t, w2_dw, w2_ds, w_dw, w_ds, f"b{t}")
+            return crossed(t, w2_dw, w2_ds, w_dw, w_ds, f"b{t}", nc.scalar.copy)
 
         def put_scalar(board, lst, src, lo, hi):
             nc.scalar.activation(board[:].indirect(lst[:, lo // 16 : hi // 16]), src[:, lo:hi], ACT.Copy)
@@ -155,33 +154,32 @@ def tile_list_crossed_shared_one_finalgate_kernel(
         def read(t, lo, hi):
             nc.vector.tensor_copy(hid[:, lo:hi, t], pages[t][:].indirect(read_list[:, lo // 16 : hi // 16]))
 
-        a0 = first_a(0)
+        a0 = first_a(0, nc.vector.tensor_copy)
         b0 = first_b(0)
-        put_vector(a_boards[0], a_list, a0, 0, J)
         a1 = first_a(1)
+        put_vector(a_boards[0], a_list, a0, 0, J)
         put_scalar(b_boards[0], b_list, b0, 0, J)
         put_vector(a_boards[1], a_list, a1, 0, J)
+        join(0, nc.gpsimd)
         b1 = first_b(1)
         a2 = first_a(2)
         put_scalar(b_boards[1], b_list, b1, 0, J)
-        join(0, nc.vector)
         put_vector(a_boards[2], a_list, a2, 0, J)
+        join(1, nc.gpsimd)
         read(0, 0, O)
         b2 = first_b(2)
         a3 = first_a(3)
         put_scalar(b_boards[2], b_list, b2, 0, J)
-        join(1, nc.vector)
-        b3 = first_b(3)
-        put_scalar(a_boards[0], a_list, a3, 0, P)
+        join(2, nc.gpsimd)
+        put_vector(a_boards[0], a_list, a3, 0, J)
         read(1, 0, O)
+        b3 = first_b(3)
         put_scalar(b_boards[0], b_list, b3, 0, J)
-        join(2, nc.vector)
-        put_vector(a_boards[0], a_list, a3, P, J)
         read(2, 0, O)
         join(3, nc.vector)
 
 
-        gate = keep.tile([P, 2, O], F32, name="gate")
+        gate = keep.tile([P, 2, O], F32, name="gate", tag="b3_sb")
         for h in range(2):
             nc.scalar.activation(
                 gate[:, h, :], tz_rows[h][:].indirect(gate_list[:]), ACT.Sigmoid,

from contextlib import ExitStack

import concourse.mybir as mybir

K, T, Z, J, R, C, O, N, E = 512, 1024, 1024, 256, 512, 512, 256, 256, 1024
FLOPS = 2 * (4 * K * R * J + R * N * O)

F32 = mybir.dt.float32
BF16 = mybir.dt.bfloat16
I32 = mybir.dt.int32
U32 = mybir.dt.uint32
U16 = mybir.dt.uint16
U8 = mybir.dt.uint8
E4M3 = mybir.dt.float8_e4m3fn_x4
E5M2 = mybir.dt.float8_e5m2_x4
E2M1 = mybir.dt.float4_e2m1fn_x4
ACT = mybir.ActivationFunctionType
ALU = mybir.AluOpType

P = 128
PACK = 4
QUADS = 4


def tile_list_crossed_shared_one_finalgate_kernel(
    tc, xt_words, xt_scales, xo_words, xo_scales, w_words, w_scales, w2_words, w2_scales,
    wb_words, wb_scales, tz, so, bo, offs, offs2, offs3, offs4, offs5, offs6, out,
):
    nc = tc.nc
    with ExitStack() as ctx:
        keep = ctx.enter_context(tc.tile_pool(name="keep", bufs=1))
        ring = ctx.enter_context(tc.tile_pool(name="ring", bufs=2))
        psum = ctx.enter_context(tc.psum_pool(name="psum", bufs=1))

        def load_list(src, name):
            tile = keep.tile([P, J // 16], U16, name=name)
            nc.sync.dma_start(tile[:], src)
            return tile

        def zeroed_scales(width, name):
            tile = keep.tile([P, width], U8, name=name, align_bytes=64)
            nc.vector.memset(tile[:].bitcast(I32), 0)
            return tile

        def load_scales(queue, tile, src):
            for q in range(QUADS):
                queue.dma_start(tile[32 * q : 32 * q + 4, :].bitcast(I32), src[0, 4 * q : 4 * q + 4, :].bitcast(I32))

        def load_words(src, width, name, tag):
            tile = keep.tile([P, width], U32, name=name, tag=tag, align_bytes=64)
            nc.sync.dma_start(tile[:].bitcast(I32), src[0].rearrange("p n t -> p (n t)").bitcast(I32))
            return tile

        xo_s = zeroed_scales(Z, "xo_s")
        xt_s = zeroed_scales(T, "xt_s")
        w_s = zeroed_scales(R, "w_s")
        w2_s = zeroed_scales(R, "w2_s")
        wb_s = zeroed_scales(N, "wb_s")

        note_list = load_list(offs2, "note_list")
        load_scales(nc.sync, xo_s, xo_scales)
        token_list = load_list(offs, "token_list")
        xo_w = keep.tile([P, Z], U16, name="xo_w", tag="table1", align_bytes=64)
        nc.sync.dma_start(xo_w[:].bitcast(I32), xo_words[0].bitcast(I32))
        xt_w = load_words(xt_words, T, "xt_w", "table0")
        load_scales(nc.sync, xt_s, xt_scales)
        w_w = load_words(w_words, R, "w_w", "w_w")
        w2_w = load_words(w2_words, R, "w2_w", "w2_w")
        load_scales(nc.sync, w_s, w_scales)
        load_scales(nc.sync, w2_s, w2_scales)
        a_list = load_list(offs3, "a_list")
        b_list = load_list(offs4, "b_list")
        read_list = load_list(offs5, "read_list")
        wb_w = load_words(wb_words, N, "wb_w", "wb_w")
        load_scales(nc.sync, wb_s, wb_scales)
        gate_list = load_list(offs6, "gate_list")
        slope = keep.tile([P, 2], F32, name="slope")
        offset = keep.tile([P, 2], F32, name="offset")
        with nc.allow_non_contiguous_dma(reason="one value a partition and half"):
            nc.sync.dma_start(slope[:], so.rearrange("(h p) o -> p (h o)", p=P))
            nc.sync.dma_start(offset[:], bo.rearrange("(h p) o -> p (h o)", p=P))

        a_boards = [keep.tile([P, C], F32, name=f"a_board{i}") for i in range(3)]
        b_boards = [keep.tile([P, C], F32, name=f"b_board{i}") for i in range(3)]
        for pair in zip(a_boards, b_boards):
            for board in pair:
                nc.vector.memset(board[:], 0.0)

        xo_gw = keep.tile([P, J], U16, name="xo_gw", align_bytes=64)
        xo_gs = keep.tile([P, J], U8, name="xo_gs", align_bytes=64)
        xt_gw = keep.tile([P, J], U32, name="xt_gw", align_bytes=64)
        xt_gs = keep.tile([P, J], U8, name="xt_gs", align_bytes=64)
        nc.vector.tensor_copy(xo_gs[:], xo_s[:].indirect(note_list[:]))
        nc.vector.tensor_copy(xo_gw[:], xo_w[:].indirect(note_list[:]))
        nc.vector.tensor_copy(xt_gw[:], xt_w[:].indirect(token_list[:]))
        nc.vector.tensor_copy(xt_gs[:], xt_s[:].indirect(token_list[:]))

        def dealt(copy, src, dtype, run, name):
            tile = keep.tile([P, PACK, P], dtype, name=name, align_bytes=64)
            copy(
                tile[:].rearrange("p t (b i) -> p b t i", i=run),
                src[:].rearrange("p (b i t) -> p b t i", i=run, t=PACK),
            )
            return tile

        w_dw = dealt(nc.scalar.copy, w_w, U32, 4, "w_dw")
        w2_dw = dealt(nc.scalar.copy, w2_w, U32, 4, "w2_dw")
        w_ds = dealt(nc.vector.tensor_copy, w_s, U8, 16, "w_ds")
        w2_ds = keep.tile([P, PACK, P], U8, name="w2_ds", align_bytes=64)
        w2_cols = w2_s[:].rearrange("p (b i t) -> p b t i", i=16, t=PACK)
        w2_dealt = w2_ds[:].rearrange("p t (b i) -> p b t i", i=16)
        nc.vector.tensor_copy(w2_dealt[:, :, 0:1, :], w2_cols[:, :, 0:1, :])
        nc.vector.tensor_copy(w2_dealt[:, :, 1:PACK, :], w2_cols[:, :, 1:PACK, :])

        tz_rows = []
        for h in range(2):
            rows = keep.tile([P, E], F32, name=f"tz{h}", tag=f"table{h}", align_bytes=64)
            nc.sync.dma_start(rows[:], tz[P * h : P * (h + 1), :])
            tz_rows.append(rows)

        def crossed(t, token_w, token_s, note_w, note_s, name, copy):
            acc = psum.tile([P, J], F32, name=name, tag="first", bufs=3)
            passes = [(token_w, token_s, xt_gw[:].bitcast(E4M3), xt_gs), (note_w, note_s, xo_gw[:].bitcast(E2M1), xo_gs)]
            if token_w is w2_dw:
                passes = passes[::-1]
            for n, (lw, ls, rw, rs) in enumerate(passes):
                nc.tensor.matmul_mx(
                    acc[:], lhsT=lw[:, t, :].bitcast(E5M2), lhsT_scale=ls[:, t, :],
                    rhs=rw, rhs_scale=rs[:], start=(n == 0), stop=(n == 1),
                )
            sb = keep.tile([P, J], F32, name=name + "_sb", tag=name + "_sb")
            copy(sb[:], acc[:])
            return sb

        def first_a(t, copy=nc.scalar.copy):
            return crossed(t, w_dw, w_ds, w2_dw, w2_ds, f"a{t}", copy)

        def first_b(t):
            return crossed(t, w2_dw, w2_ds, w_dw, w_ds, f"b{t}", nc.scalar.copy)

        def put_scalar(board, lst, src, lo, hi):
            nc.scalar.activation(board[:].indirect(lst[:, lo // 16 : hi // 16]), src[:, lo:hi], ACT.Copy)

        def put_vector(board, lst, src, lo, hi):
            nc.vector.tensor_copy(board[:].indirect(lst[:, lo // 16 : hi // 16]), src[:, lo:hi])

        hid = keep.tile([P, O, PACK], BF16, name="hid", align_bytes=64)
        pages = {}

        def join(t, engine):
            pages[t] = keep.tile([P, C], F32, name=f"page{t}")
            engine.tensor_tensor(pages[t][:], a_boards[t % 3][:], b_boards[t % 3][:], ALU.add)

        def read(t, lo, hi):
            nc.vector.tensor_copy(hid[:, lo:hi, t], pages[t][:].indirect(read_list[:, lo // 16 : hi // 16]))

        a0 = first_a(0, nc.vector.tensor_copy)
        b0 = first_b(0)
        a1 = first_a(1)
        put_vector(a_boards[0], a_list, a0, 0, J)
        put_scalar(b_boards[0], b_list, b0, 0, J)
        put_vector(a_boards[1], a_list, a1, 0, J)
        join(0, nc.gpsimd)
        b1 = first_b(1)
        a2 = first_a(2)
        put_scalar(b_boards[1], b_list, b1, 0, J)
        put_vector(a_boards[2], a_list, a2, 0, J)
        join(1, nc.gpsimd)
        read(0, 0, O)
        b2 = first_b(2)
        a3 = first_a(3)
        put_scalar(b_boards[2], b_list, b2, 0, J)
        join(2, nc.gpsimd)
        put_vector(a_boards[0], a_list, a3, 0, J)
        read(1, 0, O)
        b3 = first_b(3)
        put_scalar(b_boards[0], b_list, b3, 0, J)
        read(2, 0, O)
        join(3, nc.vector)


        gate = keep.tile([P, 2, O], F32, name="gate", tag="b3_sb")
        for h in range(2):
            nc.scalar.activation(
                gate[:, h, :], tz_rows[h][:].indirect(gate_list[:]), ACT.Sigmoid,
                bias=offset[:, h : h + 1], scale=slope[:, h : h + 1],
            )
        out_rows = out.rearrange("(h p) o -> p h o", p=P)
        read(3, 0, P)
        read(3, P, O)
        accs = []
        for u in range(2):
            cols = slice(P * u, P * (u + 1))
            hid_w = keep.tile([P, P], U32, name=f"hid_w{u}", align_bytes=64)
            hid_s = keep.tile([P, P], U8, name=f"hid_s{u}", align_bytes=64)
            nc.vector.quantize_mx(hid_w[:].bitcast(E4M3), hid_s[:], hid[:, cols, :].rearrange("p o t -> p (o t)"))
            acc = psum.tile([P, 2, P], F32, name=f"p{u}", tag="second", bufs=2)
            for h in range(2):
                rows = slice(P * h, P * (h + 1))
                nc.tensor.matmul_mx(
                    acc[:, h, :], lhsT=wb_w[:, rows].bitcast(E5M2), lhsT_scale=wb_s[:, rows],
                    rhs=hid_w[:].bitcast(E4M3), rhs_scale=hid_s[:], start=True, stop=True,
                )
            accs.append(acc)
        for u in range(2):
            cols = slice(P * u, P * (u + 1))
            y = keep.tile([P, 2, P], F32, name=f"y{u}")
            nc.vector.tensor_tensor(y[:], accs[u][:], gate[:, :, cols], ALU.mult)
            (nc.sync, nc.scalar)[u].dma_start(out_rows[:, :, cols], y[:])
